import numpy as np
import ml_dtypes


def mxq(x, axis, fmt="e4m3"):
    dtype, down = {"e4m3": (ml_dtypes.float8_e4m3fn, 7), "e5m2": (ml_dtypes.float8_e5m2, 14)}[fmt]
    v = np.moveaxis(np.asarray(x, np.float32).astype(ml_dtypes.bfloat16).astype(np.float64), axis, -1)
    blocks = v.reshape(v.shape[:-1] + (-1, 32))
    amax = np.abs(blocks).max(-1, keepdims=True)
    byte = np.maximum(np.where(amax > 0, np.frexp(amax)[1] - 1 + 127, 0) - down, 1)
    scale = np.exp2(byte - 127.0)
    codes = (blocks / scale).astype(np.float32).astype(dtype).astype(np.float64)
    return np.moveaxis((codes * scale).reshape(v.shape), -1, axis)


WIDE = False


def mx_kscale(k):
    if not WIDE:
        return np.ones(k)
    levels = np.array([10, -10, 5, -5, 0])
    if k % 512:
        return np.exp2(np.random.permutation(np.resize(levels, k // 32))).repeat(32)
    a = np.empty((k // 512, 16))
    for p in range(k // 512):
        a[p, :8] = np.random.permutation(np.resize(levels, 8))
        for g in range(8):
            far = levels[np.abs(levels - a[p, g]) >= 10]
            a[p, g + 8] = far[np.random.randint(len(far))]
    return np.exp2(a.ravel()).repeat(32)


BF16 = ml_dtypes.bfloat16


def bf(x):
    return np.asarray(x, np.float32).astype(BF16)


def f64(x):
    return np.asarray(x).astype(np.float64)


E2M1 = np.array([0.0, 0.5, 1.0, 1.5, 2.0, 3.0, 4.0, 6.0, -0.0, -0.5, -1.0, -1.5, -2.0, -3.0, -4.0, -6.0])


def pack_weight(w, fmt):
    k, n = w.shape
    w = f64(bf(w)).reshape(k // 32, 32, n)
    amax = np.abs(w).max(1)
    if fmt == "e4m3":
        byte = np.frexp(amax)[1] - 1 + 127 - 7
    else:
        mant, ex = np.frexp(amax / 6.0)
        byte = np.where(mant > 0.5, ex, ex - 1) + 127
    byte = np.clip(np.where(amax > 0, byte, 1), 1, 254)
    scaled = (w * np.exp2(127.0 - byte)[:, None, :]).reshape(k, n).astype(np.float32)
    by_word = np.ascontiguousarray(scaled.reshape(k // 512, 128, 4, n).transpose(0, 1, 3, 2))
    if fmt == "e4m3":
        words = by_word.astype(ml_dtypes.float8_e4m3fn).view(np.uint8)
    else:
        c = by_word.astype(ml_dtypes.float4_e2m1fn).view(np.uint8) & 0xF
        words = c[..., 0::2] | (c[..., 1::2] << 4)
    return np.ascontiguousarray(words), np.ascontiguousarray(byte.astype(np.uint8).reshape(k // 512, 16, n))


def unpack_weight(words, scales, fmt):
    g, p, n, _ = words.shape
    if fmt == "e4m3":
        vals = np.ascontiguousarray(words).view(ml_dtypes.float8_e4m3fn).astype(np.float64)
    else:
        nib = np.empty((g, p, n, 4), np.uint8)
        nib[..., 0::2] = words & 0xF
        nib[..., 1::2] = words >> 4
        vals = E2M1[nib]
    vals = vals * np.repeat(np.exp2(scales.astype(np.float64) - 127.0), 8, axis=1)[..., None]
    return vals.transpose(0, 1, 3, 2).reshape(g * 512, n)
def pack4(w):
    words, scales = pack_weight(w, "e2m1")
    return words.reshape(words.shape[0], 128, -1), scales


def unpack4(words, scales):
    return unpack_weight(words.reshape(words.shape[0], 128, -1, 2), scales, "e2m1")


G, M, A, F, C = 4, 512, 1024, 1024, 512


def setup_inputs():
    s = mx_kscale(G * A).reshape(G, A)
    t = mx_kscale(G * F).reshape(G, F)
    freq = np.random.uniform(-1, 1, (G, 1, F))
    phase = np.random.uniform(0, 2 * np.pi, (G, 1, F))
    d = np.sqrt(2 / A) * np.cos(np.pi * np.arange(A)[None, :, None] * freq + phase)
    d = d / s[:, :, None] * t[:, None, :]
    r = np.random.standard_normal((G, F, C)) / np.sqrt(F) / t[:, :, None]
    d_words, d_scales = pack4(d.reshape(G * A, F))
    r_words, r_scales = pack4(r.reshape(G * F, C))
    return {"x": bf(np.random.standard_normal((G, M, A)) * s[:, None, :]),
            "d_words": d_words, "d_scales": d_scales,
            "theta": bf(np.random.uniform(0.3, 0.7, (G, F)) * t),
            "r_words": r_words, "r_scales": r_scales}


def reference(x, d_words, d_scales, theta, r_words, r_scales):
    d = unpack4(d_words, d_scales).reshape(G, A, F)
    r = unpack4(r_words, r_scales).reshape(G, F, C)
    th = f64(theta)[:, None, :]
    z = mxq(f64(x), 2, "e4m3") @ d
    h = z - np.maximum(np.minimum(z, th), -th)
    y = mxq(h, 2, "e4m3") @ r
    return y

from contextlib import ExitStack

import concourse.mybir as mybir
from concourse.masks import make_identity

BANDS, TOK, ANT, ATOM, FEED = 4, 512, 1024, 1024, 512
FLOPS = 2 * BANDS * TOK * ATOM * (ANT + FEED)
BYTES = BANDS * TOK * ANT * 2 + BANDS * ANT * ATOM // 2 + BANDS * ATOM * FEED // 2 + BANDS * TOK * FEED * 4

F32 = mybir.dt.float32
BF16 = mybir.dt.bfloat16
I32 = mybir.dt.int32
U32 = mybir.dt.uint32
U8 = mybir.dt.uint8
FP8X4 = mybir.dt.float8_e4m3fn_x4
FP4X4 = mybir.dt.float4_e2m1fn_x4
ALU = mybir.AluOpType
ACT = mybir.ActivationFunctionType

P = 128

PL = {"pz":4,"pt":2,"py":2,"loads":[["xt",[0,1]],["ds",0],["xt",[1,2]],["dh",0],["xt",[2,4]],["dh",1],["sp",0],["x",1],["r",3],["d",1],["d",3],["sp",1],["x",2],["rs",0],["d",2],["r",0],["r",2],["sp",2],["x",3],["r",1],["sp",3]],"head":[["p",0],["t",0],["t",1],["cs",0],["cs",1],["q",0],["q",1],["p",1],["p",3],["t",3],["t",2],["cs",2],["q",2],["cs",3],["p",2],["q",3],["nth",0]],"T":[[3,0],[4.25,1],[4.25,2],[3.5,3]],"C":[[3,0],[4.5,1],[4.75,2],[3.5,3]],"QX":[[7,0],[7,1]],"PERM":[[5.5,0,0,"vvvv"],[6.5,0,1,"vvvv"],[11,1,0,"vvvv"],[6,1,1,"vvvv"]],"permEng":"vector","QH":[[14,0,0,512],[14,1,0,512]],"MM2":[[15.25,0],[15.25,1],[15.75,2],[17,3]],"stLag":2.25,"tail":[["il","v",256,384],["il","s",0,128],["q",256,384],["m",2],["il","g",128,256],["il","g",384,512],["y",2,"s"],["q",128,256],["q",0,128],["m",1],["m",0],["q",384,512],["m",3],["y",1,"v"],["y",3,"s"],["y",0,"s"]],"stD":0,"IL":[[7,0,0,256,"gggg"],[9,0,256,512,"gggg"],[14,1,0,256,"gggg"],[11.25,1,256,512,"gggs"]],"cE":["svsv","ssss","ssss","ssss"],"yE":["ssss","ssss","ssss","svvv"],"M0":[[21,0],[25.5,1],[18.75,2],[23.25,3]]}


def tile_csi_feedback_bands_s14_kernel(tc, x, d_words, d_scales, theta, r_words, r_scales, out):
    nc = tc.nc
    with ExitStack() as ctx:
        keep = ctx.enter_context(tc.tile_pool(name="keep", bufs=1))
        two = ctx.enter_context(tc.tile_pool(name="two", bufs=2))
        three = ctx.enter_context(tc.tile_pool(name="three", bufs=4))
        many = ctx.enter_context(tc.tile_pool(name="many", bufs=6))
        pz = ctx.enter_context(tc.psum_pool(name="pz", bufs=PL["pz"]))
        pt = ctx.enter_context(tc.psum_pool(name="pt", bufs=PL["pt"]))
        py = ctx.enter_context(tc.psum_pool(name="py", bufs=PL["py"]))
        ctx.enter_context(tc.manual_schedule())

        ident = keep.tile([P, P], F32, name="ident")
        sraw = keep.tile([P, ATOM], U8, name="sraw", align_bytes=64)
        sper = keep.tile([P, ATOM], U8, name="sper", align_bytes=64)
        rplane = keep.tile([P, 8, FEED], U8, name="rplane", align_bytes=64)
        th_bf = keep.tile([P, 8, 4], BF16, name="th_bf")
        th = keep.tile([P, 8, 4], F32, name="th")
        nth = keep.tile([P, 8, 4], F32, name="nth")
        warm = keep.tile([P, 1], F32, name="warm")
        xs, draw, dper, dplane, rw = [], [], [], [], []
        for b in range(BANDS):
            xs.append(keep.tile([P, 4, ANT], BF16, name="xs%d" % b, align_bytes=64))
            draw.append(keep.tile([P, 2, 2 * ATOM], U8, name="draw%d" % b, align_bytes=64))
            dper.append([keep.tile([P, 2, 4, 256], U8, name="dper%d_%d" % (b, h), align_bytes=64) for h in range(2)])
            dplane.append(keep.tile([P, 2, ATOM], U8, name="dplane%d" % b, align_bytes=64))
            rw.append(keep.tile([P, 2, 2 * FEED], U8, name="rw%d" % b, align_bytes=64))

        def load_x(b, whole):
            src = x[b].rearrange("(i p) a -> p i a", p=P)
            if whole:
                nc.sync.dma_start(out=xs[b][:], in_=src)
            else:
                for i in range(4):
                    nc.sync.dma_start(out=xs[b][:, i, :], in_=src[:, i, :])

        def load_d(b):
            nc.sync.dma_start(out=draw[b][:], in_=d_words[2 * b : 2 * b + 2].rearrange("g p n -> p g n"))

        def load_d_half(b, h):
            cols = slice(1024 * h, 1024 * (h + 1))
            nc.sync.dma_start(out=draw[b][:, :, cols], in_=d_words[2 * b : 2 * b + 2, :, cols].rearrange("g p n -> p g n"))

        def load_r(b):
            nc.sync.dma_start(out=rw[b][:], in_=r_words[2 * b : 2 * b + 2].rearrange("g p n -> p g n"))

        def spread_d_scales(b):
            for l in range(2):
                for q in range(4):
                    row = 32 * b + 16 * l + 4 * q
                    nc.sync.dma_start(
                        out=dplane[b][32 * q : 32 * q + 4, l, :].bitcast(I32),
                        in_=sper[row : row + 4, :].bitcast(I32),
                    )

        xg, xc, xsc, tb = {}, {}, {}, {}
        zb, rt, ht, hi, hc, hsc = {}, {}, {}, {}, {}, {}
        yb = {}

        def transposes(b, i):
            bank = pt.tile([P, 2, 2, P], F32, name="tbank")
            words = xs[b][:, i, :].bitcast(F32)
            for g in range(2):
                for u in range(2):
                    nc.tensor.transpose(bank[:, g, u, :], words[:, 256 * g + u : 256 * (g + 1) : 2], ident[:])
            tb[b, i] = bank

        def copy_t(b, i, copy):
            if i == 0:
                xg[b] = two.tile([P, 2, TOK, 4], BF16, name="xg", align_bytes=64)
            dst = xg[b][:, :, P * i : P * (i + 1), :].bitcast(F32)
            copy(out=dst, in_=tb[b, i][:].rearrange("p g u r -> p g r u"))

        def quant_x_tile(b, i):
            if i == 0:
                xc[b] = two.tile([P, 2, TOK], U32, name="xc", align_bytes=64)
                xsc[b] = two.tile([P, 2, TOK], U8, name="xsc", align_bytes=64)
            cols = slice(P * i, P * (i + 1))
            for g in range(2):
                nc.vector.quantize_mx(
                    out=xc[b][:, g, cols].bitcast(FP8X4),
                    scales=xsc[b][:, g, cols],
                    in_=xg[b][:, g, cols, :].rearrange("p n t -> p (n t)"),
                )

        def quant_x(b, g):
            if g == 0:
                xc[b] = two.tile([P, 2, TOK], U32, name="xc", align_bytes=64)
                xsc[b] = two.tile([P, 2, TOK], U8, name="xsc", align_bytes=64)
            nc.vector.quantize_mx(
                out=xc[b][:, g, :].bitcast(FP8X4),
                scales=xsc[b][:, g, :],
                in_=xg[b][:, g, :, :].rearrange("p n t -> p (n t)"),
            )

        def permute_d(b, h, g, eng):
            eng.tensor_copy(
                out=dper[b][h][:, g, :, :].rearrange("p t (m c) -> p t m c", c=2),
                in_=draw[b][:, g, 1024 * h : 1024 * (h + 1)].rearrange("p (m t c) -> p t m c", t=4, c=2),
            )

        def mm1(b, h, t):
            bank = pz.tile([P, TOK], F32, name="zbank")
            for g in range(2):
                nc.tensor.matmul_mx(
                    out=bank[:],
                    lhsT=dper[b][h][:, g, t, :].bitcast(FP4X4),
                    lhsT_scale=dplane[b][:, g, 512 * h + P * t : 512 * h + P * (t + 1)],
                    rhs=xc[b][:, g, :].bitcast(FP8X4),
                    rhs_scale=xsc[b][:, g, :],
                    start=(g == 0),
                    stop=(g == 1),
                )
            zb[b, h, t] = bank

        def relu(b, h, t):
            r = many.tile([P, TOK], BF16, name="relu_r")
            nc.scalar.activation(out=r[:], in_=zb[b, h, t][:], func=ACT.Relu, bias=nth[:, 2 * b + h, t : t + 1], scale=1.0)
            rt[b, h, t] = r

        def shrink(b, h, t):
            if t == 0:
                ht[b, h] = three.tile([P, 4, TOK], BF16, name="ht", align_bytes=64)
            nc.vector.scalar_tensor_tensor(
                out=ht[b, h][:, t, :],
                in0=zb[b, h, t][:],
                scalar=th[:, 2 * b + h, t : t + 1],
                in1=rt[b, h, t][:],
                op0=ALU.add,
                op1=ALU.min,
            )

        def interleave_views(b, h, lo, up):
            if (b, h) not in hi:
                hi[b, h] = three.tile([P, TOK, 4], BF16, name="hint", align_bytes=64)
            dst = hi[b, h][:, lo:up, :].rearrange("p (c i) t -> p c t i", i=4)
            src = ht[b, h][:, :, lo:up].rearrange("p t (c i) -> p c t i", i=4)
            return dst, src

        def interleave_v(b, h, lo, up):
            dst, src = interleave_views(b, h, lo, up)
            nc.vector.tensor_copy(out=dst, in_=src)

        def interleave_g(b, h, lo, up):
            interleave_views(b, h, lo, up)
            dst, src = hi[b, h][:, lo:up, :], ht[b, h][:, :, lo:up].rearrange("p t n -> p n t")
            nc.gpsimd.tensor_scalar(out=dst, in0=src, scalar1=1.0, scalar2=0.0, op0=ALU.mult, op1=ALU.add)

        def interleave_s(b, h, lo, up):
            dst, src = interleave_views(b, h, lo, up)
            nc.scalar.copy(out=dst, in_=src)

        def quant_h(b, h, lo, up):
            if (b, h) not in hc:
                hc[b, h] = three.tile([P, TOK], U32, name="hc", align_bytes=64)
                hsc[b, h] = three.tile([P, TOK], U8, name="hsc", align_bytes=64)
            nc.vector.quantize_mx(
                out=hc[b, h][:, lo:up].bitcast(FP8X4),
                scales=hsc[b, h][:, lo:up],
                in_=hi[b, h][:, lo:up, :].rearrange("p n t -> p (n t)"),
            )

        def mm2_pass(b, i, h):
            rows = slice(P * i, P * (i + 1))
            nc.tensor.matmul_mx(
                out=yb[b, i][:],
                lhsT=hc[b, h][:, rows].bitcast(FP8X4),
                lhsT_scale=hsc[b, h][:, rows],
                rhs=rw[b][:, h, :].bitcast(FP4X4),
                rhs_scale=rplane[:, 2 * b + h, :],
                start=(h == 0),
                stop=(h == 1),
            )

        def mm2(b, i):
            bank = py.tile([P, FEED], F32, name="ybank")
            yb[b, i] = bank
            for h in range(2):
                mm2_pass(b, i, h)

        def store(b, i, copy):
            y = many.tile([P, FEED], F32, name="ysb")
            copy(out=y[:], in_=yb[b, i][:])
            nc.sync.dma_start(out=out[b, P * i : P * (i + 1), :], in_=y[:])

        nc.vector.memset(warm[:], 0.0)
        nc.scalar.activation(out=warm[:], in_=warm[:], func=ACT.Relu)
        make_identity(nc, ident[:])
        for b in range(BANDS):
            (nc.vector if b == 0 else nc.gpsimd).memset(dplane[b][:].rearrange("p g n -> p (g n)").bitcast(I32), 0)
        nc.gpsimd.memset(rplane[:].rearrange("p g n -> p (g n)").bitcast(I32), 0)

        def load_d_scales():
            nc.sync.dma_start(out=sraw[:].bitcast(I32), in_=d_scales.rearrange("g q n -> (g q) n").bitcast(I32))

        def load_r_scales():
            for q in range(4):
                nc.sync.dma_start(
                    out=rplane[32 * q : 32 * q + 4, :, :].bitcast(I32),
                    in_=r_scales[:, 4 * q : 4 * q + 4, :].rearrange("g q n -> q g n").bitcast(I32),
                )

        nc.scalar.dma_start(out=th_bf[:], in_=theta.rearrange("b (h p t) -> p (b h) t", h=2, t=4))
        for name, arg in PL["loads"]:
            if name == "x4":
                load_x(arg, False)
            elif name == "xt":
                lo, up = arg
                nc.sync.dma_start(
                    out=xs[0][:, lo:up, :], in_=x[0].rearrange("(i p) a -> p i a", p=P)[:, lo:up, :]
                )
            elif name == "x":
                load_x(arg, True)
            elif name == "ds":
                load_d_scales()
            elif name == "d":
                load_d(arg)
            elif name == "dh":
                load_d_half(0, arg)
            elif name == "sp":
                if arg == 0:
                    nc.vector.tensor_copy(
                        out=sper[:].rearrange("p (h t m) -> p h t m", h=2, t=4),
                        in_=sraw[:].rearrange("p (h m t) -> p h t m", h=2, t=4),
                    )
                spread_d_scales(arg)
            elif name == "rs":
                load_r_scales()
            elif name == "r":
                load_r(arg)
        for name, arg in PL["head"]:
            if name == "nth":
                nc.vector.tensor_copy(out=th[:], in_=th_bf[:])
                nc.vector.tensor_scalar(out=nth[:], in0=th_bf[:], scalar1=-1.0, scalar2=None, op0=ALU.mult)
            if name == "t":
                transposes(0, arg)
            elif name == "cs":
                copy_t(0, arg, nc.scalar.copy)
            elif name == "cv":
                copy_t(0, arg, nc.vector.tensor_copy)
            elif name == "q":
                quant_x_tile(0, arg)
            elif name == "pg":
                permute_d(0, arg // 2, arg % 2, nc.gpsimd)
            elif name == "p":
                permute_d(0, arg // 2, arg % 2, nc.vector)

        def tail_first_pass(i):
            b = BANDS - 1
            if i < 2:
                bank = pt.tile([P, FEED], F32, name="tbank")
            else:
                bank = py.tile([P, FEED], F32, name="ybank")
            yb[b, i] = bank
            mm2_pass(b, i, 0)

        agenda = {}

        def at(slot, step, *args):
            agenda.setdefault(slot, []).append((step, args))

        for b in range(BANDS):
            base = 8 * b
            early = base - 8
            if b > 0:
                for k, i in PL["T"]:
                    at(early + k, transposes, b, i)
            for k in range(8):
                at(base + k, mm1, b, k // 4, k % 4)
                at(base + k, relu, b, k // 4, k % 4)
            if b > 0:
                for k, i in PL["C"]:
                    at(early + k, copy_t, b, i, nc.vector.tensor_copy if PL["cE"][b][i] == "v" else nc.scalar.copy)
            for k in range(8):
                at(base + k + PL["stLag"], shrink, b, k // 4, k % 4)
            for k, h, lo, up, eng in PL["IL"]:
                if not (b == BANDS - 1 and h == 1):
                    at(base + k, {"g": interleave_g, "v": interleave_v, "s": interleave_s}[eng[b]], b, h, lo, up)
            if b > 0:
                for k, g in PL["QX"]:
                    at(early + k, quant_x, b, g)
                for k, h, g, eng in PL["PERM"]:
                    at(early + k, permute_d, b, h, g, nc.gpsimd if eng[b] == "g" else nc.vector)
            for k, h, lo, up in PL["QH"]:
                if not (b == BANDS - 1 and h == 1):
                    at(base + k, quant_h, b, h, lo, up)
            if b < BANDS - 1:
                for k, i in PL["MM2"]:
                    at(base + k, mm2, b, i)
                    at(base + k + PL["stD"], store, b, i, nc.vector.tensor_copy if PL["yE"][b][i] == "v" else nc.scalar.copy)
        for k, i in PL["M0"]:
            at(8 * (BANDS - 1) + k, tail_first_pass, i)
        for slot in sorted(agenda):
            for step, args in agenda[slot]:
                step(*args)
        b = BANDS - 1
        for step in PL["tail"]:
            if step[0] == "il":
                if step[1] == "g":
                    interleave_g(b, 1, step[2], step[3])
                elif step[1] == "s":
                    dst, src = interleave_views(b, 1, step[2], step[3])
                    nc.scalar.copy(out=dst, in_=src)
                else:
                    interleave_v(b, 1, step[2], step[3])
            elif step[0] == "q":
                quant_h(b, 1, step[1], step[2])
            elif step[0] == "m":
                mm2_pass(b, step[1], 1)
            else:
                store(b, step[1], nc.scalar.copy if step[2] == "s" else nc.vector.tensor_copy)
